import numpy as np
import ml_dtypes


def mxq(x, axis, fmt="e4m3"):
    dtype, down = {"e4m3": (ml_dtypes.float8_e4m3fn, 7), "e5m2": (ml_dtypes.float8_e5m2, 14)}[fmt]
    v = np.moveaxis(np.asarray(x, np.float32).astype(ml_dtypes.bfloat16).astype(np.float64), axis, -1)
    blocks = v.reshape(v.shape[:-1] + (-1, 32))
    amax = np.abs(blocks).max(-1, keepdims=True)
    byte = np.maximum(np.where(amax > 0, np.frexp(amax)[1] - 1 + 127, 0) - down, 1)
    scale = np.exp2(byte - 127.0)
    codes = (blocks / scale).astype(np.float32).astype(dtype).astype(np.float64)
    return np.moveaxis((codes * scale).reshape(v.shape), -1, axis)


WIDE = False


def mx_kscale(k):
    if not WIDE:
        return np.ones(k)
    levels = np.array([10, -10, 5, -5, 0])
    if k % 512:
        return np.exp2(np.random.permutation(np.resize(levels, k // 32))).repeat(32)
    a = np.empty((k // 512, 16))
    for p in range(k // 512):
        a[p, :8] = np.random.permutation(np.resize(levels, 8))
        for g in range(8):
            far = levels[np.abs(levels - a[p, g]) >= 10]
            a[p, g + 8] = far[np.random.randint(len(far))]
    return np.exp2(a.ravel()).repeat(32)


def f64(x):
    return np.asarray(x).astype(np.float64)


def striped(idx):
    return np.tile(idx.reshape(-1, 16).T, (8, 1)).astype(np.uint16)


def unstriped(offs):
    return offs[:16].T.reshape(-1).astype(np.int64)


K, T, E, C, N = 512, 4096, 8, 256, 256


def by_expert(wq, xq):
    return np.concatenate([wq[e].T @ xq[:, e * C:(e + 1) * C] for e in range(E)], axis=1)


def setup_inputs():
    n = np.random.standard_normal
    s = mx_kscale(K)[:, None]
    return {
        "xT": (n((K, T)) * s).astype(np.float32),
        "w": (n((E, K, N)) / np.sqrt(K) / s[None]).astype(np.float32),
        "gate": np.tile(np.random.uniform(0.2, 1.0, E * C), (N, 1)).astype(np.float32),
        "offs": striped(np.random.permutation(T)[:E * C]),
    }


def reference(xT, w, gate, offs):
    idx = unstriped(offs)
    xq = mxq(f64(xT)[:, idx], 0, "e4m3")
    y = by_expert(mxq(f64(w), 1, "e4m3"), xq)
    out = np.zeros((N, T))
    out[:, idx] = f64(gate) * y
    return out

@@ -1,0 +1,136 @@
+from contextlib import ExitStack
+
+import concourse.mybir as mybir
+
+K, T, E, C, N = 512, 4096, 8, 256, 256
+SLOTS = E * C
+FLOPS = 2 * SLOTS * K * N
+BYTES = 4 * K * T + 4 * E * K * N + 4 * SLOTS + 2 * 128 * 128 + 4 * N * T
+
+F32 = mybir.dt.float32
+BF16 = mybir.dt.bfloat16
+U32 = mybir.dt.uint32
+U16 = mybir.dt.uint16
+U8 = mybir.dt.uint8
+FP8X4 = mybir.dt.float8_e4m3fn_x4
+
+P = 128
+PACK = 4
+GROUP = 512
+GROUPS = SLOTS // GROUP
+LIST_COLS = GROUP // 16
+BLOCKS = N // P
+
+X_PIECES = (
+    (0, 0, 1024, 0), (0, 1024, 1024, 1024), (0, 2048, 1024, 0), (0, 3072, 1024, 512),
+    (1, 0, 1024, 0), (1, 1024, 1024, 0), (1, 2048, 1024, 512), (1, 3072, 512, 0), (1, 3584, 512, 256),
+)
+
+
+def tile_routed_moe_kernel(tc, xT, w, gate, offs, out):
+    nc = tc.nc
+    mult = mybir.AluOpType.mult
+
+    with ExitStack() as ctx:
+        keep = ctx.enter_context(tc.tile_pool(name="keep", bufs=1))
+        xstage = ctx.enter_context(tc.tile_pool(name="xstage", bufs=5))
+        wstage = ctx.enter_context(tc.tile_pool(name="wstage", bufs=4))
+        wround = ctx.enter_context(tc.tile_pool(name="wround", bufs=2))
+        psum = ctx.enter_context(tc.psum_pool(name="psum", bufs=8))
+
+        offsets = keep.tile([P, SLOTS // 16], U16, name="offsets")
+        nc.sync.dma_start(offsets[:], offs)
+
+        windows = []
+        for b in range(BLOCKS):
+            window = keep.tile([P, T], F32, name=f"window{b}")
+            (nc.vector if b == 0 else nc.gpsimd).memset(window[:], 0.0)
+            windows.append(window)
+
+        pairs = [keep.tile([P, 2 * T], BF16, name=f"pairs{u}", align_bytes=64) for u in range(2)]
+        x_rounded = [keep.tile([P, 2 * GROUP * PACK], BF16, name=f"x_rounded{h}", align_bytes=64) for h in range(GROUPS // 2)]
+        x_codes = [keep.tile([P, GROUP], U32, name=f"x_codes{g}", align_bytes=64) for g in range(GROUPS)]
+        x_scales = [keep.tile([P, GROUP], U8, name=f"x_scales{g}", align_bytes=64) for g in range(GROUPS)]
+
+        def gather(u, g, groups):
+            words = x_rounded[g // 2][:].bitcast(U32).rearrange("p (n u) -> p n u", u=2)
+            n0 = g % 2 * GROUP
+            nc.vector.tensor_copy(
+                words[:, n0 : n0 + groups * GROUP, u],
+                pairs[u][:].bitcast(U32).indirect(offsets[:, g * LIST_COLS : (g + groups) * LIST_COLS]),
+            )
+
+        x_view = xT.rearrange("(p u e) t -> u p e t", u=2, e=2)
+        for u in range(2):
+            for piece_u, t0, tokens, on_vector in X_PIECES:
+                if piece_u != u:
+                    continue
+                raw = xstage.tile([P, 2, 1024], F32, name="raw")
+                nc.sync.dma_start(raw[:, :, :tokens], x_view[u, :, :, t0 : t0 + tokens])
+                dst = pairs[u][:].rearrange("p (t e) -> p t e", e=2)
+                src = raw[:].rearrange("p e t -> p t e")
+                cut = tokens - on_vector
+                if cut:
+                    nc.scalar.copy(dst[:, t0 : t0 + cut, :], src[:, :cut, :])
+                if on_vector:
+                    nc.vector.tensor_copy(dst[:, t0 + cut : t0 + tokens, :], src[:, cut:tokens, :])
+            if u == 0:
+                for g in range(0, GROUPS, 2):
+                    gather(0, g, 2)
+
+        gates = keep.tile([P, SLOTS], F32, name="gates")
+        w_raw = []
+        for g in range(GROUPS):
+            raw_w = wstage.tile([P, 2, PACK, N], F32, name="raw_w")
+            nc.sync.dma_start(raw_w[:], w[2 * g : 2 * g + 2].rearrange("e (p j) n -> p e j n", j=PACK))
+            w_raw.append(raw_w)
+            nc.sync.dma_start(gates[:, g * GROUP : (g + 1) * GROUP], gate[0:P, g * GROUP : (g + 1) * GROUP])
+
+        y = [keep.tile([P, SLOTS], F32, name=f"y{b}") for b in range(BLOCKS)]
+
+        def scatter(b, g0, g1):
+            slots = slice(g0 * GROUP, g1 * GROUP)
+            nc.vector.tensor_tensor(
+                windows[b][:].indirect(offsets[:, g0 * LIST_COLS : g1 * LIST_COLS]),
+                y[b][:, slots],
+                gates[:, slots],
+                mult,
+            )
+
+        for g in range(GROUPS):
+            gather(1, g, 1)
+            c0 = g % 2 * GROUP * PACK
+            nc.vector.quantize_mx(
+                out=x_codes[g][:].bitcast(FP8X4), scales=x_scales[g][:], in_=x_rounded[g // 2][:, c0 : c0 + GROUP * PACK]
+            )
+
+        for g in range(GROUPS):
+            rounded_w = wround.tile([P, 2, N, PACK], BF16, name="rounded_w", align_bytes=64)
+            for e in range(2):
+                nc.scalar.copy(rounded_w[:, e], w_raw[g][:, e].rearrange("p j n -> p n j"))
+            w_codes = keep.tile([P, 2 * N], U32, name=f"w_codes{g}", align_bytes=64)
+            w_scales = keep.tile([P, 2 * N], U8, name=f"w_scales{g}", align_bytes=64)
+            nc.vector.quantize_mx(
+                out=w_codes[:].bitcast(FP8X4), scales=w_scales[:], in_=rounded_w[:].rearrange("p e n j -> p (e n j)")
+            )
+            for b in range(BLOCKS):
+                bank = psum.tile([P, GROUP], F32, name="bank")
+                for e in range(2):
+                    slots = slice(e * C, (e + 1) * C)
+                    cols = slice(e * N + b * P, e * N + (b + 1) * P)
+                    nc.tensor.matmul_mx(
+                        out=bank[:, slots],
+                        lhsT=w_codes[:, cols].bitcast(FP8X4),
+                        lhsT_scale=w_scales[:, cols],
+                        rhs=x_codes[g][:, slots].bitcast(FP8X4),
+                        rhs_scale=x_scales[g][:, slots],
+                        start=True,
+                        stop=True,
+                    )
+                nc.scalar.copy(y[b][:, g * GROUP : (g + 1) * GROUP], bank[:])
+            scatter(0, g, g + 1)
+            if g == 0:
+                scatter(1, 0, 1)
+        nc.sync.dma_start(out[0:P, :], windows[0][:])
+        scatter(1, 1, GROUPS)
+        nc.sync.dma_start(out[P : 2 * P, :], windows[1][:])

@@ -21,9 +21,11 @@ GROUPS = SLOTS // GROUP
 LIST_COLS = GROUP // 16
 BLOCKS = N // P
 
+GATE_CUTS = (0, GROUP, SLOTS)
+
 X_PIECES = (
     (0, 0, 1024, 0), (0, 1024, 1024, 1024), (0, 2048, 1024, 0), (0, 3072, 1024, 512),
-    (1, 0, 1024, 0), (1, 1024, 1024, 0), (1, 2048, 1024, 512), (1, 3072, 512, 0), (1, 3584, 512, 256),
+    (1, 0, 1024, 0), (1, 1024, 1024, 0), (1, 2048, 1024, 512), (1, 3072, 512, 256), (1, 3584, 512, 352),
 )
 
 
@@ -34,12 +36,9 @@ def tile_routed_moe_kernel(tc, xT, w, gate, offs, out):
     with ExitStack() as ctx:
         keep = ctx.enter_context(tc.tile_pool(name="keep", bufs=1))
         xstage = ctx.enter_context(tc.tile_pool(name="xstage", bufs=5))
-        wstage = ctx.enter_context(tc.tile_pool(name="wstage", bufs=4))
+        wstage = ctx.enter_context(tc.tile_pool(name="wstage", bufs=8))
         wround = ctx.enter_context(tc.tile_pool(name="wround", bufs=2))
         psum = ctx.enter_context(tc.psum_pool(name="psum", bufs=8))
-
-        offsets = keep.tile([P, SLOTS // 16], U16, name="offsets")
-        nc.sync.dma_start(offsets[:], offs)
 
         windows = []
         for b in range(BLOCKS):
@@ -47,46 +46,17 @@ def tile_routed_moe_kernel(tc, xT, w, gate, offs, out):
             (nc.vector if b == 0 else nc.gpsimd).memset(window[:], 0.0)
             windows.append(window)
 
+        offsets = keep.tile([P, SLOTS // 16], U16, name="offsets")
         pairs = [keep.tile([P, 2 * T], BF16, name=f"pairs{u}", align_bytes=64) for u in range(2)]
-        x_rounded = [keep.tile([P, 2 * GROUP * PACK], BF16, name=f"x_rounded{h}", align_bytes=64) for h in range(GROUPS // 2)]
-        x_codes = [keep.tile([P, GROUP], U32, name=f"x_codes{g}", align_bytes=64) for g in range(GROUPS)]
-        x_scales = [keep.tile([P, GROUP], U8, name=f"x_scales{g}", align_bytes=64) for g in range(GROUPS)]
-
-        def gather(u, g, groups):
-            words = x_rounded[g // 2][:].bitcast(U32).rearrange("p (n u) -> p n u", u=2)
-            n0 = g % 2 * GROUP
-            nc.vector.tensor_copy(
-                words[:, n0 : n0 + groups * GROUP, u],
-                pairs[u][:].bitcast(U32).indirect(offsets[:, g * LIST_COLS : (g + groups) * LIST_COLS]),
-            )
-
-        x_view = xT.rearrange("(p u e) t -> u p e t", u=2, e=2)
-        for u in range(2):
-            for piece_u, t0, tokens, on_vector in X_PIECES:
-                if piece_u != u:
-                    continue
-                raw = xstage.tile([P, 2, 1024], F32, name="raw")
-                nc.sync.dma_start(raw[:, :, :tokens], x_view[u, :, :, t0 : t0 + tokens])
-                dst = pairs[u][:].rearrange("p (t e) -> p t e", e=2)
-                src = raw[:].rearrange("p e t -> p t e")
-                cut = tokens - on_vector
-                if cut:
-                    nc.scalar.copy(dst[:, t0 : t0 + cut, :], src[:, :cut, :])
-                if on_vector:
-                    nc.vector.tensor_copy(dst[:, t0 + cut : t0 + tokens, :], src[:, cut:tokens, :])
-            if u == 0:
-                for g in range(0, GROUPS, 2):
-                    gather(0, g, 2)
-
+        x_rounded = keep.tile([P, SLOTS * PACK], BF16, name="x_rounded", align_bytes=64)
+        x_codes = keep.tile([P, SLOTS], U32, name="x_codes", align_bytes=64)
+        x_scales = keep.tile([P, SLOTS], U8, name="x_scales", align_bytes=64)
         gates = keep.tile([P, SLOTS], F32, name="gates")
-        w_raw = []
-        for g in range(GROUPS):
-            raw_w = wstage.tile([P, 2, PACK, N], F32, name="raw_w")
-            nc.sync.dma_start(raw_w[:], w[2 * g : 2 * g + 2].rearrange("e (p j) n -> p e j n", j=PACK))
-            w_raw.append(raw_w)
-            nc.sync.dma_start(gates[:, g * GROUP : (g + 1) * GROUP], gate[0:P, g * GROUP : (g + 1) * GROUP])
-
         y = [keep.tile([P, SLOTS], F32, name=f"y{b}") for b in range(BLOCKS)]
+
+        def gather(u):
+            words = x_rounded[:].bitcast(U32).rearrange("p (n u) -> p n u", u=2)
+            nc.vector.tensor_copy(words[:, :, u], pairs[u][:].bitcast(U32).indirect(offsets[:]))
 
         def scatter(b, g0, g1):
             slots = slice(g0 * GROUP, g1 * GROUP)
@@ -97,40 +67,79 @@ def tile_routed_moe_kernel(tc, xT, w, gate, offs, out):
                 mult,
             )
 
-        for g in range(GROUPS):
-            gather(1, g, 1)
-            c0 = g % 2 * GROUP * PACK
+        x_view = xT.rearrange("(p u e) t -> u p e t", u=2, e=2)
+        for u in range(2):
+            for piece_u, t0, tokens, on_vector in X_PIECES:
+                if piece_u != u:
+                    continue
+                raw = xstage.tile([P, 2, 1024], F32, name="raw")
+                nc.sync.dma_start(raw[:, :, :tokens], x_view[u, :, :, t0 : t0 + tokens])
+                if u == 0 and t0 == 0:
+                    nc.sync.dma_start(offsets[:], offs)
+                dst = pairs[u][:].rearrange("p (t e) -> p t e", e=2)
+                src = raw[:].rearrange("p e t -> p t e")
+                cut = tokens - on_vector
+                if cut:
+                    nc.scalar.copy(dst[:, t0 : t0 + cut, :], src[:, :cut, :])
+                if on_vector:
+                    nc.vector.tensor_copy(dst[:, t0 + cut : t0 + tokens, :], src[:, cut:tokens, :])
+            if u == 0:
+                gather(0)
+
+        HALF = E // 2
+        w_codes, w_scales = [], []
+        for h in range(2):
+            rounded_w = wround.tile([P, HALF, N, PACK], BF16, name="rounded_w", align_bytes=64)
+            for e in range(HALF):
+                raw_w = wstage.tile([P, PACK, N], F32, name="raw_w")
+                nc.sync.dma_start(raw_w[:], w[h * HALF + e].rearrange("(p j) n -> p j n", j=PACK))
+                src = raw_w[:].rearrange("p j n -> p n j")
+                if h * HALF + e == E - 1:
+                    nc.vector.tensor_copy(rounded_w[:, e], src)
+                else:
+                    nc.scalar.copy(rounded_w[:, e], src)
+            codes = keep.tile([P, HALF * N], U32, name=f"w_codes{h}", align_bytes=64)
+            scales = keep.tile([P, HALF * N], U8, name=f"w_scales{h}", align_bytes=64)
             nc.vector.quantize_mx(
-                out=x_codes[g][:].bitcast(FP8X4), scales=x_scales[g][:], in_=x_rounded[g // 2][:, c0 : c0 + GROUP * PACK]
+                out=codes[:].bitcast(FP8X4), scales=scales[:], in_=rounded_w[:].rearrange("p e n j -> p (e n j)")
+            )
+            w_codes.append(codes)
+            w_scales.append(scales)
+            nc.sync.dma_start(gates[:, GATE_CUTS[h] : GATE_CUTS[h + 1]], gate[0:P, GATE_CUTS[h] : GATE_CUTS[h + 1]])
+
+        gather(1)
+        for h in range(2):
+            slots = slice(h * HALF * C, (h + 1) * HALF * C)
+            nc.vector.quantize_mx(
+                out=x_codes[:, slots].bitcast(FP8X4),
+                scales=x_scales[:, slots],
+                in_=x_rounded[:, h * HALF * C * PACK : (h + 1) * HALF * C * PACK],
             )
 
-        for g in range(GROUPS):
-            rounded_w = wround.tile([P, 2, N, PACK], BF16, name="rounded_w", align_bytes=64)
-            for e in range(2):
-                nc.scalar.copy(rounded_w[:, e], w_raw[g][:, e].rearrange("p j n -> p n j"))
-            w_codes = keep.tile([P, 2 * N], U32, name=f"w_codes{g}", align_bytes=64)
-            w_scales = keep.tile([P, 2 * N], U8, name=f"w_scales{g}", align_bytes=64)
-            nc.vector.quantize_mx(
-                out=w_codes[:].bitcast(FP8X4), scales=w_scales[:], in_=rounded_w[:].rearrange("p e n j -> p (e n j)")
-            )
-            for b in range(BLOCKS):
-                bank = psum.tile([P, GROUP], F32, name="bank")
-                for e in range(2):
+        for b in range(BLOCKS):
+            for i in range(HALF):
+                bank = psum.tile([P, 2, C], F32, name="bank")
+                for h in range(2):
+                    e = h * HALF + i
                     slots = slice(e * C, (e + 1) * C)
-                    cols = slice(e * N + b * P, e * N + (b + 1) * P)
+                    cols = slice(i * N + b * P, i * N + (b + 1) * P)
                     nc.tensor.matmul_mx(
-                        out=bank[:, slots],
-                        lhsT=w_codes[:, cols].bitcast(FP8X4),
-                        lhsT_scale=w_scales[:, cols],
-                        rhs=x_codes[g][:, slots].bitcast(FP8X4),
-                        rhs_scale=x_scales[g][:, slots],
+                        out=bank[:, h, :],
+                        lhsT=w_codes[h][:, cols].bitcast(FP8X4),
+                        lhsT_scale=w_scales[h][:, cols],
+                        rhs=x_codes[:, slots].bitcast(FP8X4),
+                        rhs_scale=x_scales[:, slots],
                         start=True,
                         stop=True,
                     )
-                nc.scalar.copy(y[b][:, g * GROUP : (g + 1) * GROUP], bank[:])
-            scatter(0, g, g + 1)
-            if g == 0:
-                scatter(1, 0, 1)
+                dst = y[b][:].rearrange("p (h i c) -> p i h c", h=2, i=HALF)[:, i]
+                if b == 0 and i == 1:
+                    nc.vector.tensor_copy(dst, bank[:])
+                else:
+                    nc.scalar.copy(dst, bank[:])
+
+        scatter(0, 0, 1)
+        scatter(0, 1, GROUPS)
         nc.sync.dma_start(out[0:P, :], windows[0][:])
-        scatter(1, 1, GROUPS)
+        scatter(1, 0, GROUPS)
         nc.sync.dma_start(out[P : 2 * P, :], windows[1][:])

@@ -24,7 +24,7 @@ BLOCKS = N // P
 GATE_CUTS = (0, GROUP, SLOTS)
 
 X_PIECES = (
-    (0, 0, 1024, 0), (0, 1024, 1024, 1024), (0, 2048, 1024, 0), (0, 3072, 1024, 512),
+    (0, 0, 2048, 896), (0, 2048, 2048, 896),
     (1, 0, 1024, 0), (1, 1024, 1024, 0), (1, 2048, 1024, 512), (1, 3072, 512, 256), (1, 3584, 512, 352),
 )
 
@@ -35,9 +35,9 @@ def tile_routed_moe_kernel(tc, xT, w, gate, offs, out):
 
     with ExitStack() as ctx:
         keep = ctx.enter_context(tc.tile_pool(name="keep", bufs=1))
-        xstage = ctx.enter_context(tc.tile_pool(name="xstage", bufs=5))
-        wstage = ctx.enter_context(tc.tile_pool(name="wstage", bufs=8))
-        wround = ctx.enter_context(tc.tile_pool(name="wround", bufs=2))
+        xstage = ctx.enter_context(tc.tile_pool(name="xstage", bufs=4))
+        wstage = ctx.enter_context(tc.tile_pool(name="wstage", bufs=4))
+        shared = ctx.enter_context(tc.tile_pool(name="shared", bufs=1))
         psum = ctx.enter_context(tc.psum_pool(name="psum", bufs=8))
 
         windows = []
@@ -49,8 +49,6 @@ def tile_routed_moe_kernel(tc, xT, w, gate, offs, out):
         offsets = keep.tile([P, SLOTS // 16], U16, name="offsets")
         pairs = [keep.tile([P, 2 * T], BF16, name=f"pairs{u}", align_bytes=64) for u in range(2)]
         x_rounded = keep.tile([P, SLOTS * PACK], BF16, name="x_rounded", align_bytes=64)
-        x_codes = keep.tile([P, SLOTS], U32, name="x_codes", align_bytes=64)
-        x_scales = keep.tile([P, SLOTS], U8, name="x_scales", align_bytes=64)
         gates = keep.tile([P, SLOTS], F32, name="gates")
         y = [keep.tile([P, SLOTS], F32, name=f"y{b}") for b in range(BLOCKS)]
 
@@ -72,7 +70,7 @@ def tile_routed_moe_kernel(tc, xT, w, gate, offs, out):
             for piece_u, t0, tokens, on_vector in X_PIECES:
                 if piece_u != u:
                     continue
-                raw = xstage.tile([P, 2, 1024], F32, name="raw")
+                raw = xstage.tile([P, 2, (2048, 1024)[u]], F32, name=f"raw{u}", bufs=(2, 4)[u])
                 nc.sync.dma_start(raw[:, :, :tokens], x_view[u, :, :, t0 : t0 + tokens])
                 if u == 0 and t0 == 0:
                     nc.sync.dma_start(offsets[:], offs)
@@ -87,59 +85,52 @@ def tile_routed_moe_kernel(tc, xT, w, gate, offs, out):
                 gather(0)
 
         HALF = E // 2
-        w_codes, w_scales = [], []
+        gather(1)
+        w_rounded = []
         for h in range(2):
-            rounded_w = wround.tile([P, HALF, N, PACK], BF16, name="rounded_w", align_bytes=64)
+            rounded_w = shared.tile([P, HALF, N, PACK], BF16, name=("first", "second")[h], align_bytes=64)
             for e in range(HALF):
                 raw_w = wstage.tile([P, PACK, N], F32, name="raw_w")
                 nc.sync.dma_start(raw_w[:], w[h * HALF + e].rearrange("(p j) n -> p j n", j=PACK))
-                src = raw_w[:].rearrange("p j n -> p n j")
-                if h * HALF + e == E - 1:
-                    nc.vector.tensor_copy(rounded_w[:, e], src)
-                else:
-                    nc.scalar.copy(rounded_w[:, e], src)
+                nc.scalar.copy(rounded_w[:, e], raw_w[:].rearrange("p j n -> p n j"))
+            w_rounded.append(rounded_w)
+            nc.sync.dma_start(gates[:, GATE_CUTS[h] : GATE_CUTS[h + 1]], gate[0:P, GATE_CUTS[h] : GATE_CUTS[h + 1]])
+
+        for h in range(2):
             codes = keep.tile([P, HALF * N], U32, name=f"w_codes{h}", align_bytes=64)
             scales = keep.tile([P, HALF * N], U8, name=f"w_scales{h}", align_bytes=64)
             nc.vector.quantize_mx(
-                out=codes[:].bitcast(FP8X4), scales=scales[:], in_=rounded_w[:].rearrange("p e n j -> p (e n j)")
+                out=codes[:].bitcast(FP8X4), scales=scales[:], in_=w_rounded[h][:].rearrange("p e n j -> p (e n j)")
             )
-            w_codes.append(codes)
-            w_scales.append(scales)
-            nc.sync.dma_start(gates[:, GATE_CUTS[h] : GATE_CUTS[h + 1]], gate[0:P, GATE_CUTS[h] : GATE_CUTS[h + 1]])
-
-        gather(1)
-        for h in range(2):
-            slots = slice(h * HALF * C, (h + 1) * HALF * C)
+            x_codes = shared.tile([P, HALF * C], U32, name=("third", "first")[h], align_bytes=64)
+            x_scales = keep.tile([P, HALF * C], U8, name=f"x_scales{h}", align_bytes=64)
             nc.vector.quantize_mx(
-                out=x_codes[:, slots].bitcast(FP8X4),
-                scales=x_scales[:, slots],
+                out=x_codes[:].bitcast(FP8X4),
+                scales=x_scales[:],
                 in_=x_rounded[:, h * HALF * C * PACK : (h + 1) * HALF * C * PACK],
             )
-
-        for b in range(BLOCKS):
-            for i in range(HALF):
-                bank = psum.tile([P, 2, C], F32, name="bank")
-                for h in range(2):
-                    e = h * HALF + i
-                    slots = slice(e * C, (e + 1) * C)
-                    cols = slice(i * N + b * P, i * N + (b + 1) * P)
-                    nc.tensor.matmul_mx(
-                        out=bank[:, h, :],
-                        lhsT=w_codes[h][:, cols].bitcast(FP8X4),
-                        lhsT_scale=w_scales[h][:, cols],
-                        rhs=x_codes[:, slots].bitcast(FP8X4),
-                        rhs_scale=x_scales[:, slots],
-                        start=True,
-                        stop=True,
-                    )
-                dst = y[b][:].rearrange("p (h i c) -> p i h c", h=2, i=HALF)[:, i]
-                if b == 0 and i == 1:
-                    nc.vector.tensor_copy(dst, bank[:])
-                else:
-                    nc.scalar.copy(dst, bank[:])
+            for b in range(BLOCKS):
+                for i in range(HALF // 2):
+                    bank = psum.tile([P, 2, C], F32, name="bank")
+                    e0 = h * HALF + 2 * i
+                    for j in range(2):
+                        cols = slice((2 * i + j) * N + b * P, (2 * i + j) * N + (b + 1) * P)
+                        slots = slice((2 * i + j) * C, (2 * i + j + 1) * C)
+                        nc.tensor.matmul_mx(
+                            out=bank[:, j, :],
+                            lhsT=codes[:, cols].bitcast(FP8X4),
+                            lhsT_scale=scales[:, cols],
+                            rhs=x_codes[:, slots].bitcast(FP8X4),
+                            rhs_scale=x_scales[:, slots],
+                            start=True,
+                            stop=True,
+                        )
+                    nc.scalar.copy(y[b][:, e0 * C : (e0 + 2) * C], bank[:].rearrange("p j n -> p (j n)"))
 
         scatter(0, 0, 1)
-        scatter(0, 1, GROUPS)
+        scatter(0, 1, 2)
+        scatter(1, 0, 2)
+        scatter(0, 2, 4)
         nc.sync.dma_start(out[0:P, :], windows[0][:])
-        scatter(1, 0, GROUPS)
+        scatter(1, 2, GROUPS)
         nc.sync.dma_start(out[P : 2 * P, :], windows[1][:])

@@ -21,10 +21,8 @@ GROUPS = SLOTS // GROUP
 LIST_COLS = GROUP // 16
 BLOCKS = N // P
 
-GATE_CUTS = (0, GROUP, SLOTS)
-
 X_PIECES = (
-    (0, 0, 2048, 896), (0, 2048, 2048, 896),
+    (0, 0, 2048, 896), (0, 2048, 1024, 448), (0, 3072, 512, 256), (0, 3584, 512, 352),
     (1, 0, 1024, 0), (1, 1024, 1024, 0), (1, 2048, 1024, 512), (1, 3072, 512, 256), (1, 3584, 512, 352),
 )
 
@@ -50,7 +48,7 @@ def tile_routed_moe_kernel(tc, xT, w, gate, offs, out):
         pairs = [keep.tile([P, 2 * T], BF16, name=f"pairs{u}", align_bytes=64) for u in range(2)]
         x_rounded = keep.tile([P, SLOTS * PACK], BF16, name="x_rounded", align_bytes=64)
         gates = keep.tile([P, SLOTS], F32, name="gates")
-        y = [keep.tile([P, SLOTS], F32, name=f"y{b}") for b in range(BLOCKS)]
+        y = [[None, None] for b in range(BLOCKS)]
 
         def gather(u):
             words = x_rounded[:].bitcast(U32).rearrange("p (n u) -> p n u", u=2)
@@ -60,7 +58,7 @@ def tile_routed_moe_kernel(tc, xT, w, gate, offs, out):
             slots = slice(g0 * GROUP, g1 * GROUP)
             nc.vector.tensor_tensor(
                 windows[b][:].indirect(offsets[:, g0 * LIST_COLS : g1 * LIST_COLS]),
-                y[b][:, slots],
+                y[b][g0 // 2][:, g0 % 2 * GROUP : (g0 % 2 + g1 - g0) * GROUP],
                 gates[:, slots],
                 mult,
             )
@@ -70,7 +68,7 @@ def tile_routed_moe_kernel(tc, xT, w, gate, offs, out):
             for piece_u, t0, tokens, on_vector in X_PIECES:
                 if piece_u != u:
                     continue
-                raw = xstage.tile([P, 2, (2048, 1024)[u]], F32, name=f"raw{u}", bufs=(2, 4)[u])
+                raw = xstage.tile([P, 2, max(tokens, 1024)], F32, name=f"raw{max(tokens, 1024)}", bufs=1 if tokens > 1024 else 5)
                 nc.sync.dma_start(raw[:, :, :tokens], x_view[u, :, :, t0 : t0 + tokens])
                 if u == 0 and t0 == 0:
                     nc.sync.dma_start(offsets[:], offs)
@@ -94,43 +92,58 @@ def tile_routed_moe_kernel(tc, xT, w, gate, offs, out):
                 nc.sync.dma_start(raw_w[:], w[h * HALF + e].rearrange("(p j) n -> p j n", j=PACK))
                 nc.scalar.copy(rounded_w[:, e], raw_w[:].rearrange("p j n -> p n j"))
             w_rounded.append(rounded_w)
-            nc.sync.dma_start(gates[:, GATE_CUTS[h] : GATE_CUTS[h + 1]], gate[0:P, GATE_CUTS[h] : GATE_CUTS[h + 1]])
+            half = slice(h * HALF * C, (h + 1) * HALF * C)
+            nc.sync.dma_start(gates[:, half], gate[0:P, half])
 
-        for h in range(2):
-            codes = keep.tile([P, HALF * N], U32, name=f"w_codes{h}", align_bytes=64)
+        def quantize_w(h, codes):
             scales = keep.tile([P, HALF * N], U8, name=f"w_scales{h}", align_bytes=64)
             nc.vector.quantize_mx(
                 out=codes[:].bitcast(FP8X4), scales=scales[:], in_=w_rounded[h][:].rearrange("p e n j -> p (e n j)")
             )
-            x_codes = shared.tile([P, HALF * C], U32, name=("third", "first")[h], align_bytes=64)
-            x_scales = keep.tile([P, HALF * C], U8, name=f"x_scales{h}", align_bytes=64)
+            return codes, scales
+
+        def quantize_x(h, codes):
+            scales = keep.tile([P, HALF * C], U8, name=f"x_scales{h}", align_bytes=64)
             nc.vector.quantize_mx(
-                out=x_codes[:].bitcast(FP8X4),
-                scales=x_scales[:],
+                out=codes[:].bitcast(FP8X4),
+                scales=scales[:],
                 in_=x_rounded[:, h * HALF * C * PACK : (h + 1) * HALF * C * PACK],
             )
-            for b in range(BLOCKS):
-                for i in range(HALF // 2):
-                    bank = psum.tile([P, 2, C], F32, name="bank")
-                    e0 = h * HALF + 2 * i
-                    for j in range(2):
-                        cols = slice((2 * i + j) * N + b * P, (2 * i + j) * N + (b + 1) * P)
-                        slots = slice((2 * i + j) * C, (2 * i + j + 1) * C)
-                        nc.tensor.matmul_mx(
-                            out=bank[:, j, :],
-                            lhsT=codes[:, cols].bitcast(FP8X4),
-                            lhsT_scale=scales[:, cols],
-                            rhs=x_codes[:, slots].bitcast(FP8X4),
-                            rhs_scale=x_scales[:, slots],
-                            start=True,
-                            stop=True,
-                        )
-                    nc.scalar.copy(y[b][:, e0 * C : (e0 + 2) * C], bank[:].rearrange("p j n -> p (j n)"))
+            return codes, scales
 
+        def multiply(h, b, w_mx, x_mx):
+            for i in range(HALF // 2):
+                bank = psum.tile([P, 2, C], F32, name="bank")
+                for j in range(2):
+                    cols = slice((2 * i + j) * N + b * P, (2 * i + j) * N + (b + 1) * P)
+                    slots = slice((2 * i + j) * C, (2 * i + j + 1) * C)
+                    nc.tensor.matmul_mx(
+                        out=bank[:, j, :],
+                        lhsT=w_mx[0][:, cols].bitcast(FP8X4),
+                        lhsT_scale=w_mx[1][:, cols],
+                        rhs=x_mx[0][:, slots].bitcast(FP8X4),
+                        rhs_scale=x_mx[1][:, slots],
+                        start=True,
+                        stop=True,
+                    )
+                nc.scalar.copy(y[b][h][:, 2 * i * C : (2 * i + 2) * C], bank[:].rearrange("p j n -> p (j n)"))
+
+        w0 = quantize_w(0, keep.tile([P, HALF * N], U32, name="w_codes0", align_bytes=64))
+        x0 = quantize_x(0, keep.tile([P, HALF * C], U32, name="x_codes0", align_bytes=64))
+        x1 = quantize_x(1, shared.tile([P, HALF * C], U32, name="first", align_bytes=64))
+        y[0][0] = shared.tile([P, HALF * C], F32, name="third", align_bytes=64)
+        y[1][0] = keep.tile([P, HALF * C], F32, name="y10", align_bytes=64)
+        y[0][1] = keep.tile([P, HALF * C], F32, name="y01", align_bytes=64)
+        y[1][1] = keep.tile([P, HALF * C], F32, name="y11", align_bytes=64)
+        for b in range(BLOCKS):
+            multiply(0, b, w0, x0)
         scatter(0, 0, 1)
         scatter(0, 1, 2)
+        w1 = quantize_w(1, shared.tile([P, HALF * N], U32, name="third", align_bytes=64))
+        for b in range(BLOCKS):
+            multiply(1, b, w1, x1)
         scatter(1, 0, 2)
         scatter(0, 2, 4)
         nc.sync.dma_start(out[0:P, :], windows[0][:])
-        scatter(1, 2, GROUPS)
+        scatter(1, 2, 4)
         nc.sync.dma_start(out[P : 2 * P, :], windows[1][:])

from contextlib import ExitStack

import concourse.mybir as mybir

K, T, E, C, N = 512, 4096, 8, 256, 256
SLOTS = E * C
FLOPS = 2 * SLOTS * K * N
BYTES = 4 * K * T + 4 * E * K * N + 4 * SLOTS + 2 * 128 * 128 + 4 * N * T

F32 = mybir.dt.float32
BF16 = mybir.dt.bfloat16
U32 = mybir.dt.uint32
U16 = mybir.dt.uint16
U8 = mybir.dt.uint8
FP8X4 = mybir.dt.float8_e4m3fn_x4

P = 128
PACK = 4
GROUP = 512
GROUPS = SLOTS // GROUP
LIST_COLS = GROUP // 16
BLOCKS = N // P

X_PIECES = (
    (0, 0, 2048, 896), (0, 2048, 1024, 448), (0, 3072, 512, 256), (0, 3584, 512, 352),
    (1, 0, 1024, 0), (1, 1024, 1024, 0), (1, 2048, 1024, 512), (1, 3072, 512, 256), (1, 3584, 512, 352),
)


def tile_routed_moe_kernel(tc, xT, w, gate, offs, out):
    nc = tc.nc
    mult = mybir.AluOpType.mult

    with ExitStack() as ctx:
        keep = ctx.enter_context(tc.tile_pool(name="keep", bufs=1))
        xstage = ctx.enter_context(tc.tile_pool(name="xstage", bufs=4))
        wstage = ctx.enter_context(tc.tile_pool(name="wstage", bufs=4))
        shared = ctx.enter_context(tc.tile_pool(name="shared", bufs=1))
        psum = ctx.enter_context(tc.psum_pool(name="psum", bufs=8))

        windows = []
        for b in range(BLOCKS):
            window = keep.tile([P, T], F32, name=f"window{b}")
            (nc.vector if b == 0 else nc.gpsimd).memset(window[:], 0.0)
            windows.append(window)

        offsets = keep.tile([P, SLOTS // 16], U16, name="offsets")
        pairs = [keep.tile([P, 2 * T], BF16, name=f"pairs{u}", align_bytes=64) for u in range(2)]
        x_rounded = keep.tile([P, SLOTS * PACK], BF16, name="x_rounded", align_bytes=64)
        gates = keep.tile([P, SLOTS], F32, name="gates")
        y = [[None, None] for b in range(BLOCKS)]

        def gather(u):
            words = x_rounded[:].bitcast(U32).rearrange("p (n u) -> p n u", u=2)
            nc.vector.tensor_copy(words[:, :, u], pairs[u][:].bitcast(U32).indirect(offsets[:]))

        def scatter(b, g0, g1):
            slots = slice(g0 * GROUP, g1 * GROUP)
            nc.vector.tensor_tensor(
                windows[b][:].indirect(offsets[:, g0 * LIST_COLS : g1 * LIST_COLS]),
                y[b][g0 // 2][:, g0 % 2 * GROUP : (g0 % 2 + g1 - g0) * GROUP],
                gates[:, slots],
                mult,
            )

        x_view = xT.rearrange("(p u e) t -> u p e t", u=2, e=2)
        for u in range(2):
            for piece_u, t0, tokens, on_vector in X_PIECES:
                if piece_u != u:
                    continue
                raw = xstage.tile([P, 2, max(tokens, 1024)], F32, name=f"raw{max(tokens, 1024)}", bufs=1 if tokens > 1024 else 5)
                nc.sync.dma_start(raw[:, :, :tokens], x_view[u, :, :, t0 : t0 + tokens])
                if u == 0 and t0 == 0:
                    nc.sync.dma_start(offsets[:], offs)
                dst = pairs[u][:].rearrange("p (t e) -> p t e", e=2)
                src = raw[:].rearrange("p e t -> p t e")
                cut = tokens - on_vector
                if cut:
                    nc.scalar.copy(dst[:, t0 : t0 + cut, :], src[:, :cut, :])
                if on_vector:
                    nc.vector.tensor_copy(dst[:, t0 + cut : t0 + tokens, :], src[:, cut:tokens, :])
            if u == 0:
                gather(0)

        HALF = E // 2
        gather(1)
        w_rounded = []
        for h in range(2):
            rounded_w = shared.tile([P, HALF, N, PACK], BF16, name=("first", "second")[h], align_bytes=64)
            for e in range(HALF):
                raw_w = wstage.tile([P, PACK, N], F32, name="raw_w")
                nc.sync.dma_start(raw_w[:], w[h * HALF + e].rearrange("(p j) n -> p j n", j=PACK))
                nc.scalar.copy(rounded_w[:, e], raw_w[:].rearrange("p j n -> p n j"))
            w_rounded.append(rounded_w)
            half = slice(h * HALF * C, (h + 1) * HALF * C)
            nc.sync.dma_start(gates[:, half], gate[0:P, half])

        def quantize_w(h, codes):
            scales = keep.tile([P, HALF * N], U8, name=f"w_scales{h}", align_bytes=64)
            nc.vector.quantize_mx(
                out=codes[:].bitcast(FP8X4), scales=scales[:], in_=w_rounded[h][:].rearrange("p e n j -> p (e n j)")
            )
            return codes, scales

        def quantize_x(h, codes):
            scales = keep.tile([P, HALF * C], U8, name=f"x_scales{h}", align_bytes=64)
            nc.vector.quantize_mx(
                out=codes[:].bitcast(FP8X4),
                scales=scales[:],
                in_=x_rounded[:, h * HALF * C * PACK : (h + 1) * HALF * C * PACK],
            )
            return codes, scales

        def multiply(h, b, w_mx, x_mx):
            for i in range(HALF // 2):
                bank = psum.tile([P, 2, C], F32, name="bank")
                for j in range(2):
                    cols = slice((2 * i + j) * N + b * P, (2 * i + j) * N + (b + 1) * P)
                    slots = slice((2 * i + j) * C, (2 * i + j + 1) * C)
                    nc.tensor.matmul_mx(
                        out=bank[:, j, :],
                        lhsT=w_mx[0][:, cols].bitcast(FP8X4),
                        lhsT_scale=w_mx[1][:, cols],
                        rhs=x_mx[0][:, slots].bitcast(FP8X4),
                        rhs_scale=x_mx[1][:, slots],
                        start=True,
                        stop=True,
                    )
                nc.scalar.copy(y[b][h][:, 2 * i * C : (2 * i + 2) * C], bank[:].rearrange("p j n -> p (j n)"))

        w0 = quantize_w(0, keep.tile([P, HALF * N], U32, name="w_codes0", align_bytes=64))
        x0 = quantize_x(0, keep.tile([P, HALF * C], U32, name="x_codes0", align_bytes=64))
        x1 = quantize_x(1, shared.tile([P, HALF * C], U32, name="first", align_bytes=64))
        y[0][0] = shared.tile([P, HALF * C], F32, name="third", align_bytes=64)
        y[1][0] = keep.tile([P, HALF * C], F32, name="y10", align_bytes=64)
        y[0][1] = keep.tile([P, HALF * C], F32, name="y01", align_bytes=64)
        y[1][1] = keep.tile([P, HALF * C], F32, name="y11", align_bytes=64)
        for b in range(BLOCKS):
            multiply(0, b, w0, x0)
        scatter(0, 0, 1)
        scatter(0, 1, 2)
        w1 = quantize_w(1, shared.tile([P, HALF * N], U32, name="third", align_bytes=64))
        for b in range(BLOCKS):
            multiply(1, b, w1, x1)
        scatter(1, 0, 2)
        scatter(0, 2, 4)
        nc.sync.dma_start(out[0:P, :], windows[0][:])
        scatter(1, 2, 4)
        nc.sync.dma_start(out[P : 2 * P, :], windows[1][:])
